import numpy as np
import ml_dtypes


def mxq(x, axis, fmt="e4m3"):
    dtype, down = {"e4m3": (ml_dtypes.float8_e4m3fn, 7), "e5m2": (ml_dtypes.float8_e5m2, 14)}[fmt]
    v = np.moveaxis(np.asarray(x, np.float32).astype(ml_dtypes.bfloat16).astype(np.float64), axis, -1)
    blocks = v.reshape(v.shape[:-1] + (-1, 32))
    amax = np.abs(blocks).max(-1, keepdims=True)
    byte = np.maximum(np.where(amax > 0, np.frexp(amax)[1] - 1 + 127, 0) - down, 1)
    scale = np.exp2(byte - 127.0)
    codes = (blocks / scale).astype(np.float32).astype(dtype).astype(np.float64)
    return np.moveaxis((codes * scale).reshape(v.shape), -1, axis)


WIDE = False


def mx_kscale(k):
    if not WIDE:
        return np.ones(k)
    levels = np.array([10, -10, 5, -5, 0])
    if k % 512:
        return np.exp2(np.random.permutation(np.resize(levels, k // 32))).repeat(32)
    a = np.empty((k // 512, 16))
    for p in range(k // 512):
        a[p, :8] = np.random.permutation(np.resize(levels, 8))
        for g in range(8):
            far = levels[np.abs(levels - a[p, g]) >= 10]
            a[p, g + 8] = far[np.random.randint(len(far))]
    return np.exp2(a.ravel()).repeat(32)


def f64(x):
    return np.asarray(x).astype(np.float64)


def striped(idx):
    return np.tile(idx.reshape(-1, 16).T, (8, 1)).astype(np.uint16)


def unstriped(offs):
    return offs[:16].T.reshape(-1).astype(np.int64)


def pack_weight(w):
    k, n = w.shape
    w = f64(np.asarray(w, np.float32).astype(ml_dtypes.bfloat16)).reshape(k // 32, 32, n)
    amax = np.abs(w).max(1)
    byte = np.clip(np.where(amax > 0, np.frexp(amax)[1] - 1 + 127 - 7, 1), 1, 254)
    scaled = (w * np.exp2(127.0 - byte)[:, None, :]).reshape(k, n).astype(np.float32)
    words = np.ascontiguousarray(scaled.reshape(k // 512, 128, 4, n).transpose(0, 1, 3, 2)).astype(ml_dtypes.float8_e4m3fn).view(np.uint8)
    return words, np.ascontiguousarray(byte.astype(np.uint8).reshape(k // 512, 16, n))


def unpack_weight(words, scales):
    g, p, n, _ = words.shape
    vals = np.ascontiguousarray(words).view(ml_dtypes.float8_e4m3fn).astype(np.float64) * np.repeat(np.exp2(scales.astype(np.float64) - 127.0), 8, axis=1)[..., None]
    return vals.transpose(0, 1, 3, 2).reshape(g * 512, n)


def relu2(v):
    return np.maximum(v, 0.0) ** 2


K, T, E, C, N = 2048, 768, 24, 128, 128
TOP = 4


def by_expert(wq, xq):
    return np.concatenate([wq[e].T @ xq[:, e * C:(e + 1) * C] for e in range(E)], axis=1)


def setup_inputs():
    n = np.random.standard_normal
    s = mx_kscale(K)[:, None]
    deal = np.repeat(np.arange(E), C).reshape(TOP, T)[:, np.random.permutation(T)]
    deal = np.take_along_axis(deal, np.argsort(np.random.rand(TOP, T), axis=0), axis=0)
    for _ in range(8):
        s_, t_ = np.random.permutation(T).reshape(2, -1); r = np.random.randint(TOP, size=T // 2); x, y = deal[r, s_].copy(), deal[r, t_].copy()
        ok = ~((deal[:, s_] == y).any(0) | (deal[:, t_] == x).any(0)); deal[r[ok], s_[ok]] = y[ok]; deal[r[ok], t_[ok]] = x[ok]
    order = np.lexsort((np.random.rand(TOP * T), deal.reshape(-1)))
    slot_token = order % T; pos = np.empty(TOP * T, np.int64); pos[order] = np.arange(TOP * T); pos = pos.reshape(TOP, T)
    g = np.random.uniform(0.5, 1.5, (TOP, T)); g = g / g.sum(0)
    packed = [pack_weight(m) for m in n((E, K, N)) / np.sqrt(K) / s[None]]
    return {
        "xT": (n((K, T)) * s).astype(np.float32),
        "w_words": np.stack([m[0] for m in packed]),
        "w_scales": np.stack([m[1] for m in packed]),
        "b": (0.3 * n((N, E))).astype(np.float32),
        "gate": np.stack([np.tile(r, (N, 1)) for r in g]).astype(np.float32),
        "offs": striped(slot_token),
        "pos1": striped(pos[0]),
        "pos2": striped(pos[1]),
        "pos3": striped(pos[2]),
        "pos4": striped(pos[3]),
    }


def reference(xT, w_words, w_scales, b, gate, offs, pos1, pos2, pos3, pos4):
    idx = unstriped(offs)
    w = np.stack([unpack_weight(w_words[e], w_scales[e]) for e in range(E)])
    xq = mxq(f64(xT)[:, idx], 0, "e4m3")
    y = by_expert(w, xq)
    y = relu2(y + np.repeat(f64(b), C, axis=1))
    return sum(f64(gate[r]) * y[:, unstriped(p)] for r, p in enumerate((pos1, pos2, pos3, pos4)))

@@ -1,0 +1,217 @@
+from contextlib import ExitStack
+
+import concourse.mybir as mybir
+
+F32 = mybir.dt.float32
+BF16 = mybir.dt.bfloat16
+I32 = mybir.dt.int32
+U32 = mybir.dt.uint32
+U16 = mybir.dt.uint16
+U8 = mybir.dt.uint8
+FP8X4 = mybir.dt.float8_e4m3fn_x4
+COPY = mybir.ActivationFunctionType.Copy
+RELU = mybir.ActivationFunctionType.Relu
+SQUARE = mybir.ActivationFunctionType.Square
+ADD = mybir.AluOpType.add
+MULT = mybir.AluOpType.mult
+MAX = mybir.AluOpType.max
+
+P = 128
+K, T, E, C, N, TOP = 2048, 768, 24, 128, 128, 4
+S = E * C
+PASSES = K // 512
+WINDOW = 2048
+FLOPS = 2 * K * N * S
+
+W_EXPERTS = 3
+HEAD_TOKENS = 256
+
+
+def tile_moe_tk_lin_relu2_kernel(tc, xT, w_words, w_scales, b, gate, offs, pos1, pos2, pos3, pos4, out):
+    nc = tc.nc
+    with ExitStack() as ctx:
+        keep = ctx.enter_context(tc.tile_pool(name="keep", bufs=1))
+        stage = ctx.enter_context(tc.tile_pool(name="stage", bufs=2))
+        psum = ctx.enter_context(tc.psum_pool(name="psum", bufs=8))
+
+        offs_sb = keep.tile([P, S // 16], U16, name="offs_sb")
+        pos_sb = [keep.tile([P, T // 16], U16, name=f"pos_sb{r}") for r in range(TOP)]
+        bias = keep.tile([P, E], F32, name="bias")
+        gates = keep.tile([P, TOP, T], F32, name="gates")
+        w_codes = [keep.tile([P, W_EXPERTS * PASSES * N * 4], U8, name=f"w_codes{c}", align_bytes=64) for c in range(E // W_EXPERTS)]
+        w_bytes = keep.tile([P, E * N], U8, name="w_bytes", align_bytes=64)
+        words = [keep.tile([P, WINDOW], I32, name=f"words{a}", align_bytes=64) for a in range(PASSES)]
+        scales = keep.tile([P, WINDOW], U8, name="scales", align_bytes=64)
+        slot_words = [keep.tile([P, S], U32, name=f"slot_words{a}", align_bytes=64) for a in range(PASSES)]
+        slot_scales = keep.tile([P, S], U8, name="slot_scales", align_bytes=64)
+        y = keep.tile([P, S], F32, name="y")
+
+        heads = []
+        for c in range(T // HEAD_TOKENS):
+            t0 = c * HEAD_TOKENS
+            head = keep.tile([P, 4, HEAD_TOKENS], F32, name=f"head{c}")
+            nc.sync.dma_start(head[:], xT[0:512, t0 : t0 + HEAD_TOKENS].rearrange("(p j) t -> p j t", j=4))
+            heads.append(head)
+
+        nc.gpsimd.memset(scales[:], 0)
+        nc.gpsimd.memset(w_bytes[:].bitcast(I32), 0)
+        for a in range(PASSES):
+            nc.vector.memset(words[a][:, T:WINDOW], 0)
+
+        def load_w_scales(a):
+            for q in range(4):
+                p0 = 32 * q + 4 * a
+                nc.sync.dma_start(
+                    w_bytes[p0 : p0 + 4, :].bitcast(I32).rearrange("q (e n) -> q e n", e=E),
+                    w_scales[:, a, 4 * q : 4 * q + 4, :].rearrange("e q n -> q e n").bitcast(I32),
+                )
+
+        nc.sync.dma_start(offs_sb[:], offs)
+        raws = [None]
+        for a in range(1, PASSES):
+            raw = stage.tile([P, 4, T], F32, name="raw")
+            nc.sync.dma_start(raw[:], xT[512 * a : 512 * a + 512, :].rearrange("(p j) t -> p j t", j=4))
+            raws.append(raw)
+            if a == 1:
+                nc.sync.dma_start(bias[:], b)
+            load_w_scales(a - 1)
+        for c in range(E // W_EXPERTS):
+            nc.sync.dma_start(
+                w_codes[c][:].bitcast(I32).rearrange("p (m n) -> p m n", n=N),
+                w_words[c * W_EXPERTS : (c + 1) * W_EXPERTS].rearrange("e a p n r -> p (e a) (n r)").bitcast(I32),
+            )
+            if c == 0:
+                load_w_scales(3)
+        for r, pos in enumerate((pos1, pos2, pos3, pos4)):
+            nc.sync.dma_start(pos_sb[r][:], pos)
+        nc.sync.dma_start(gates[:], gate.rearrange("r p t -> p r t"))
+
+        def cast(engine, grouped, raw, t0, t1, base):
+            dst = grouped[:, 4 * t0 : 4 * t1].rearrange("p (c i j) -> p c j i", i=4, j=4)
+            source = raw[:, :, t0 - base : t1 - base].rearrange("p j (c i) -> p c j i", i=4)
+            if engine == "scalar":
+                nc.scalar.activation(dst, source, COPY)
+            else:
+                nc.vector.tensor_copy(dst, source)
+
+        def quantize(a, grouped, t0, t1):
+            nc.vector.quantize_mx(
+                out=words[a][:, t0:t1].bitcast(FP8X4),
+                scales=scales[4 * a : P, t0:t1],
+                in_=grouped[:, 4 * t0 : 4 * t1],
+            )
+
+        def gather_words(a, s0, s1):
+            nc.vector.tensor_copy(
+                slot_words[a][:, s0:s1], words[a][:].bitcast(U32).indirect(offs_sb[:, s0 // 16 : s1 // 16])
+            )
+
+        def gather_scales(s0, s1):
+            nc.vector.tensor_copy(slot_scales[:, s0:s1], scales[:].indirect(offs_sb[:, s0 // 16 : s1 // 16]))
+
+        def multiply(acc, e, a):
+            cols = slice(e * C, (e + 1) * C)
+            m = (e % W_EXPERTS) * PASSES + a
+            nc.tensor.matmul_mx(
+                out=acc[:],
+                lhsT=w_codes[e // W_EXPERTS][:, m * N * 4 : (m + 1) * N * 4].bitcast(FP8X4),
+                lhsT_scale=w_bytes[4 * a : P, e * N : (e + 1) * N],
+                rhs=slot_words[a][:, cols].bitcast(FP8X4),
+                rhs_scale=slot_scales[4 * a : P, cols],
+                start=(a == 0),
+                stop=(a == PASSES - 1),
+            )
+
+        def finish(accs, experts):
+            e0 = experts[0]
+            relu = stage.tile([P, 4 * C], F32, name="relu")
+            for i, e in enumerate(experts):
+                nc.scalar.activation(relu[:, i * C : (i + 1) * C], accs[e][:], RELU, bias=bias[:, e : e + 1])
+            n = len(experts)
+            nc.scalar.activation(y[:, e0 * C : (e0 + n) * C], relu[:, 0 : n * C], SQUARE)
+
+        grouped = stage.tile([P, 4 * T], BF16, name="grouped", align_bytes=64)
+        cast("scalar", grouped, heads[0], 0, 256, 0)
+        cast("vector", grouped, heads[1], 256, 512, 256)
+        quantize(0, grouped, 0, 256)
+        quantize(0, grouped, 256, 512)
+        cast("vector", grouped, heads[2], 512, 672, 512)
+        cast("scalar", grouped, heads[2], 672, 768, 512)
+        quantize(0, grouped, 512, 768)
+        gather_words(0, 0, 1536)
+        gather_words(0, 1536, 2560)
+
+        def cast_and_quantize(a):
+            grouped = stage.tile([P, 4 * T], BF16, name="grouped", align_bytes=64)
+            cast("scalar", grouped, raws[a], 0, 512, 0)
+            cast("scalar", grouped, raws[a], 512, 768, 0)
+            quantize(a, grouped, 0, 512)
+            quantize(a, grouped, 512, 768)
+
+        cast_and_quantize(1)
+        gather_words(0, 2560, 3072)
+        gather_words(1, 0, 1536)
+        cast_and_quantize(2)
+        gather_words(1, 1536, 2560)
+        gather_words(2, 0, 1536)
+        cast_and_quantize(3)
+        gather_words(2, 1536, 2560)
+        gather_scales(0, 1536)
+        gather_words(3, 0, 1536)
+        accs = {}
+        for e0 in range(0, 12, 4):
+            for e in range(e0, e0 + 4):
+                accs[e] = psum.tile([P, C], F32, name="acc")
+                for a in range(PASSES):
+                    multiply(accs[e], e, a)
+            finish(accs, list(range(e0, e0 + 4)))
+        gather_scales(1536, 3072)
+        gather_words(3, 1536, 2560)
+        for e0 in range(12, 20, 4):
+            for e in range(e0, e0 + 4):
+                accs[e] = psum.tile([P, C], F32, name="acc")
+                for a in range(PASSES):
+                    multiply(accs[e], e, a)
+            finish(accs, list(range(e0, e0 + 4)))
+        gather_words(1, 2560, 3072)
+        gather_words(2, 2560, 3072)
+        for e in range(20, 24):
+            accs[e] = psum.tile([P, C], F32, name="acc")
+            for a in range(3):
+                multiply(accs[e], e, a)
+        gather_words(3, 2560, 2816)
+        multiply(accs[20], 20, 3)
+        multiply(accs[21], 21, 3)
+        finish(accs, [20, 21])
+        gather_words(3, 2816, 3072)
+        multiply(accs[23], 23, 3)
+        multiply(accs[22], 22, 3)
+        finish(accs, [22])
+        last = keep.tile([P, C], F32, name="last")
+        nc.vector.tensor_scalar(last[:], accs[23][:], bias[:, 23:24], 0.0, ADD, MAX)
+        nc.vector.tensor_tensor(y[:, 23 * C : 24 * C], last[:], last[:], MULT)
+
+        def pick(r, t0, t1):
+            prod = keep.tile([P, t1 - t0], F32, name=f"prod{r}_{t0}")
+            nc.vector.tensor_tensor(prod[:], y[:].indirect(pos_sb[r][:, t0 // 16 : t1 // 16]), gates[:, r, t0:t1], MULT)
+            return prod
+
+        def add(x, z, t0, t1, n):
+            total = keep.tile([P, t1 - t0], F32, name=f"sum{n}_{t0}")
+            nc.vector.tensor_tensor(total[:], x[:], z[:], ADD)
+            return total
+
+        a_part, b_part = (0, 512), (512, 768)
+        p = [pick(r, *a_part) for r in range(TOP)]
+        q = [pick(0, *b_part)]
+        s12 = add(p[0], p[1], *a_part, 0)
+        q.append(pick(1, *b_part))
+        s123 = add(s12, p[2], *a_part, 1)
+        q.append(pick(2, *b_part))
+        total = add(s123, p[3], *a_part, 2)
+        nc.sync.dma_start(out[:, 0:512], total[:])
+        q12 = add(q[0], q[1], *b_part, 0)
+        q.append(pick(3, *b_part))
+        q123 = add(q12, q[2], *b_part, 1)
+        total_b = add(q123, q[3], *b_part, 2)
+        nc.sync.dma_start(out[:, 512:768], total_b[:])

@@ -37,7 +37,6 @@ def tile_moe_tk_lin_relu2_kernel(tc, xT, w_words, w_scales, b, gate, offs, pos1,
         offs_sb = keep.tile([P, S // 16], U16, name="offs_sb")
         pos_sb = [keep.tile([P, T // 16], U16, name=f"pos_sb{r}") for r in range(TOP)]
         bias = keep.tile([P, E], F32, name="bias")
-        gates = keep.tile([P, TOP, T], F32, name="gates")
         w_codes = [keep.tile([P, W_EXPERTS * PASSES * N * 4], U8, name=f"w_codes{c}", align_bytes=64) for c in range(E // W_EXPERTS)]
         w_bytes = keep.tile([P, E * N], U8, name="w_bytes", align_bytes=64)
         words = [keep.tile([P, WINDOW], I32, name=f"words{a}", align_bytes=64) for a in range(PASSES)]
@@ -61,29 +60,29 @@ def tile_moe_tk_lin_relu2_kernel(tc, xT, w_words, w_scales, b, gate, offs, pos1,
         def load_w_scales(a):
             for q in range(4):
                 p0 = 32 * q + 4 * a
-                nc.sync.dma_start(
+                nc.gpsimd.dma_start(
                     w_bytes[p0 : p0 + 4, :].bitcast(I32).rearrange("q (e n) -> q e n", e=E),
                     w_scales[:, a, 4 * q : 4 * q + 4, :].rearrange("e q n -> q e n").bitcast(I32),
                 )
 
+        for a in range(PASSES):
+            load_w_scales(a)
         nc.sync.dma_start(offs_sb[:], offs)
         raws = [None]
         for a in range(1, PASSES):
-            raw = stage.tile([P, 4, T], F32, name="raw")
+            raw = stage.tile([P, 4, T], F32, name=f"raw{a}", tag="raw", bufs=3)
             nc.sync.dma_start(raw[:], xT[512 * a : 512 * a + 512, :].rearrange("(p j) t -> p j t", j=4))
             raws.append(raw)
             if a == 1:
                 nc.sync.dma_start(bias[:], b)
-            load_w_scales(a - 1)
         for c in range(E // W_EXPERTS):
             nc.sync.dma_start(
                 w_codes[c][:].bitcast(I32).rearrange("p (m n) -> p m n", n=N),
                 w_words[c * W_EXPERTS : (c + 1) * W_EXPERTS].rearrange("e a p n r -> p (e a) (n r)").bitcast(I32),
             )
-            if c == 0:
-                load_w_scales(3)
         for r, pos in enumerate((pos1, pos2, pos3, pos4)):
             nc.sync.dma_start(pos_sb[r][:], pos)
+        gates = stage.tile([P, TOP, T], F32, name="gates", tag="raw", bufs=3)
         nc.sync.dma_start(gates[:], gate.rearrange("r p t -> p r t"))
 
         def cast(engine, grouped, raw, t0, t1, base):
@@ -139,7 +138,7 @@ def tile_moe_tk_lin_relu2_kernel(tc, xT, w_words, w_scales, b, gate, offs, pos1,
         cast("scalar", grouped, heads[2], 672, 768, 512)
         quantize(0, grouped, 512, 768)
         gather_words(0, 0, 1536)
-        gather_words(0, 1536, 2560)
+        gather_words(0, 1536, 3072)
 
         def cast_and_quantize(a):
             grouped = stage.tile([P, 4 * T], BF16, name="grouped", align_bytes=64)
@@ -149,10 +148,9 @@ def tile_moe_tk_lin_relu2_kernel(tc, xT, w_words, w_scales, b, gate, offs, pos1,
             quantize(a, grouped, 512, 768)
 
         cast_and_quantize(1)
-        gather_words(0, 2560, 3072)
         gather_words(1, 0, 1536)
         cast_and_quantize(2)
-        gather_words(1, 1536, 2560)
+        gather_words(1, 1536, 3072)
         gather_words(2, 0, 1536)
         cast_and_quantize(3)
         gather_words(2, 1536, 2560)
@@ -173,7 +171,6 @@ def tile_moe_tk_lin_relu2_kernel(tc, xT, w_words, w_scales, b, gate, offs, pos1,
                 for a in range(PASSES):
                     multiply(accs[e], e, a)
             finish(accs, list(range(e0, e0 + 4)))
-        gather_words(1, 2560, 3072)
         gather_words(2, 2560, 3072)
         for e in range(20, 24):
             accs[e] = psum.tile([P, C], F32, name="acc")
@@ -193,25 +190,17 @@ def tile_moe_tk_lin_relu2_kernel(tc, xT, w_words, w_scales, b, gate, offs, pos1,
 
         def pick(r, t0, t1):
             prod = keep.tile([P, t1 - t0], F32, name=f"prod{r}_{t0}")
-            nc.vector.tensor_tensor(prod[:], y[:].indirect(pos_sb[r][:, t0 // 16 : t1 // 16]), gates[:, r, t0:t1], MULT)
+            nc.vector.tensor_tensor(prod[:], y[:].indirect(pos_sb[r][:]), gates[:, r, t0:t1], MULT)
             return prod
 
-        def add(x, z, t0, t1, n):
-            total = keep.tile([P, t1 - t0], F32, name=f"sum{n}_{t0}")
-            nc.vector.tensor_tensor(total[:], x[:], z[:], ADD)
-            return total
-
-        a_part, b_part = (0, 512), (512, 768)
-        p = [pick(r, *a_part) for r in range(TOP)]
-        q = [pick(0, *b_part)]
-        s12 = add(p[0], p[1], *a_part, 0)
-        q.append(pick(1, *b_part))
-        s123 = add(s12, p[2], *a_part, 1)
-        q.append(pick(2, *b_part))
-        total = add(s123, p[3], *a_part, 2)
-        nc.sync.dma_start(out[:, 0:512], total[:])
-        q12 = add(q[0], q[1], *b_part, 0)
-        q.append(pick(3, *b_part))
-        q123 = add(q12, q[2], *b_part, 1)
-        total_b = add(q123, q[3], *b_part, 2)
-        nc.sync.dma_start(out[:, 512:768], total_b[:])
+        p = [pick(r, 0, T) for r in range(TOP)]
+        cut = 512
+        low = keep.tile([P, T], F32, name="low")
+        high = keep.tile([P, T], F32, name="high")
+        total = keep.tile([P, T], F32, name="total")
+        nc.vector.tensor_tensor(low[:], p[0][:], p[1][:], ADD)
+        for t0, t1 in ((0, cut), (cut, T)):
+            nc.vector.tensor_tensor(high[:, t0:t1], p[2][:, t0:t1], p[3][:, t0:t1], ADD)
+        for t0, t1 in ((0, cut), (cut, T)):
+            nc.vector.tensor_tensor(total[:, t0:t1], low[:, t0:t1], high[:, t0:t1], ADD)
+            nc.sync.dma_start(out[:, t0:t1], total[:, t0:t1])

@@ -20,11 +20,11 @@ P = 128
 K, T, E, C, N, TOP = 2048, 768, 24, 128, 128, 4
 S = E * C
 PASSES = K // 512
-WINDOW = 2048
+WINDOWS = (2048, 1408, 1408, 1408)
+SCALE_WINDOW = 1408
 FLOPS = 2 * K * N * S
 
 W_EXPERTS = 3
-HEAD_TOKENS = 256
 
 
 def tile_moe_tk_lin_relu2_kernel(tc, xT, w_words, w_scales, b, gate, offs, pos1, pos2, pos3, pos4, out):
@@ -38,35 +38,24 @@ def tile_moe_tk_lin_relu2_kernel(tc, xT, w_words, w_scales, b, gate, offs, pos1,
         pos_sb = [keep.tile([P, T // 16], U16, name=f"pos_sb{r}") for r in range(TOP)]
         bias = keep.tile([P, E], F32, name="bias")
         w_codes = [keep.tile([P, W_EXPERTS * PASSES * N * 4], U8, name=f"w_codes{c}", align_bytes=64) for c in range(E // W_EXPERTS)]
-        w_bytes = keep.tile([P, E * N], U8, name="w_bytes", align_bytes=64)
-        words = [keep.tile([P, WINDOW], I32, name=f"words{a}", align_bytes=64) for a in range(PASSES)]
-        scales = keep.tile([P, WINDOW], U8, name="scales", align_bytes=64)
+        w_bytes = keep.tile([P, E * PASSES * N], U8, name="w_bytes", align_bytes=64)
+        words = [keep.tile([P, WINDOWS[a]], I32, name=f"words{a}", align_bytes=64) for a in range(PASSES)]
+        scales = keep.tile([P, SCALE_WINDOW], U8, name="scales", align_bytes=64)
         slot_words = [keep.tile([P, S], U32, name=f"slot_words{a}", align_bytes=64) for a in range(PASSES)]
         slot_scales = keep.tile([P, S], U8, name="slot_scales", align_bytes=64)
         y = keep.tile([P, S], F32, name="y")
 
         heads = []
-        for c in range(T // HEAD_TOKENS):
-            t0 = c * HEAD_TOKENS
-            head = keep.tile([P, 4, HEAD_TOKENS], F32, name=f"head{c}")
-            nc.sync.dma_start(head[:], xT[0:512, t0 : t0 + HEAD_TOKENS].rearrange("(p j) t -> p j t", j=4))
+        for t0, t1 in ((0, 512), (512, T)):
+            head = keep.tile([P, 4, t1 - t0], F32, name=f"head{t0}")
+            nc.sync.dma_start(head[:], xT[0:512, t0:t1].rearrange("(p j) t -> p j t", j=4))
             heads.append(head)
 
-        nc.gpsimd.memset(scales[:], 0)
+        nc.vector.memset(scales[:].bitcast(I32), 0)
         nc.gpsimd.memset(w_bytes[:].bitcast(I32), 0)
         for a in range(PASSES):
-            nc.vector.memset(words[a][:, T:WINDOW], 0)
+            nc.vector.memset(words[a][:, T : WINDOWS[a]], 0)
 
-        def load_w_scales(a):
-            for q in range(4):
-                p0 = 32 * q + 4 * a
-                nc.gpsimd.dma_start(
-                    w_bytes[p0 : p0 + 4, :].bitcast(I32).rearrange("q (e n) -> q e n", e=E),
-                    w_scales[:, a, 4 * q : 4 * q + 4, :].rearrange("e q n -> q e n").bitcast(I32),
-                )
-
-        for a in range(PASSES):
-            load_w_scales(a)
         nc.sync.dma_start(offs_sb[:], offs)
         raws = [None]
         for a in range(1, PASSES):
@@ -75,6 +64,11 @@ def tile_moe_tk_lin_relu2_kernel(tc, xT, w_words, w_scales, b, gate, offs, pos1,
             raws.append(raw)
             if a == 1:
                 nc.sync.dma_start(bias[:], b)
+        for q in range(4):
+            nc.sync.dma_start(
+                w_bytes[32 * q : 32 * q + 4, :].bitcast(I32).rearrange("q (m n) -> q m n", m=E * PASSES),
+                w_scales[:, :, 4 * q : 4 * q + 4, :].rearrange("e a q n -> q (e a) n").bitcast(I32),
+            )
         for c in range(E // W_EXPERTS):
             nc.sync.dma_start(
                 w_codes[c][:].bitcast(I32).rearrange("p (m n) -> p m n", n=N),
@@ -114,7 +108,7 @@ def tile_moe_tk_lin_relu2_kernel(tc, xT, w_words, w_scales, b, gate, offs, pos1,
             nc.tensor.matmul_mx(
                 out=acc[:],
                 lhsT=w_codes[e // W_EXPERTS][:, m * N * 4 : (m + 1) * N * 4].bitcast(FP8X4),
-                lhsT_scale=w_bytes[4 * a : P, e * N : (e + 1) * N],
+                lhsT_scale=w_bytes[:, (e * PASSES + a) * N : (e * PASSES + a + 1) * N],
                 rhs=slot_words[a][:, cols].bitcast(FP8X4),
                 rhs_scale=slot_scales[4 * a : P, cols],
                 start=(a == 0),
@@ -130,12 +124,11 @@ def tile_moe_tk_lin_relu2_kernel(tc, xT, w_words, w_scales, b, gate, offs, pos1,
             nc.scalar.activation(y[:, e0 * C : (e0 + n) * C], relu[:, 0 : n * C], SQUARE)
 
         grouped = stage.tile([P, 4 * T], BF16, name="grouped", align_bytes=64)
-        cast("scalar", grouped, heads[0], 0, 256, 0)
-        cast("vector", grouped, heads[1], 256, 512, 256)
-        quantize(0, grouped, 0, 256)
-        quantize(0, grouped, 256, 512)
-        cast("vector", grouped, heads[2], 512, 672, 512)
-        cast("scalar", grouped, heads[2], 672, 768, 512)
+        cast("scalar", grouped, heads[0], 0, 160, 0)
+        cast("vector", grouped, heads[0], 160, 512, 0)
+        quantize(0, grouped, 0, 512)
+        cast("vector", grouped, heads[1], 512, 672, 512)
+        cast("scalar", grouped, heads[1], 672, 768, 512)
         quantize(0, grouped, 512, 768)
         gather_words(0, 0, 1536)
         gather_words(0, 1536, 3072)
@@ -147,39 +140,45 @@ def tile_moe_tk_lin_relu2_kernel(tc, xT, w_words, w_scales, b, gate, offs, pos1,
             quantize(a, grouped, 0, 512)
             quantize(a, grouped, 512, 768)
 
-        cast_and_quantize(1)
-        gather_words(1, 0, 1536)
-        cast_and_quantize(2)
-        gather_words(1, 1536, 3072)
-        gather_words(2, 0, 1536)
-        cast_and_quantize(3)
-        gather_words(2, 1536, 2560)
-        gather_scales(0, 1536)
-        gather_words(3, 0, 1536)
         accs = {}
-        for e0 in range(0, 12, 4):
-            for e in range(e0, e0 + 4):
+
+        def first_passes(experts, passes):
+            for e in experts:
                 accs[e] = psum.tile([P, C], F32, name="acc")
-                for a in range(PASSES):
+                for a in passes:
                     multiply(accs[e], e, a)
+
+        cast_and_quantize(1)
+        gather_words(1, 0, 1024)
+        cast_and_quantize(2)
+        gather_words(1, 1024, 2048)
+        gather_words(2, 0, 1024)
+        cast_and_quantize(3)
+        gather_scales(0, 1024)
+        gather_words(3, 0, 1024)
+        for e0 in (0, 4):
+            first_passes(range(e0, e0 + 4), range(4))
             finish(accs, list(range(e0, e0 + 4)))
-        gather_scales(1536, 3072)
-        gather_words(3, 1536, 2560)
-        for e0 in range(12, 20, 4):
-            for e in range(e0, e0 + 4):
-                accs[e] = psum.tile([P, C], F32, name="acc")
-                for a in range(PASSES):
-                    multiply(accs[e], e, a)
+        gather_words(2, 1024, 2048)
+        gather_scales(1024, 2048)
+        gather_words(3, 1024, 2048)
+        for e0 in (8, 12):
+            first_passes(range(e0, e0 + 4), range(4))
             finish(accs, list(range(e0, e0 + 4)))
-        gather_words(2, 2560, 3072)
-        for e in range(20, 24):
-            accs[e] = psum.tile([P, C], F32, name="acc")
-            for a in range(3):
-                multiply(accs[e], e, a)
+        gather_words(1, 2048, 2560)
+        gather_words(2, 2048, 2560)
+        gather_scales(2048, 2560)
+        gather_words(3, 2048, 2560)
+        first_passes(range(16, 20), range(4))
+        finish(accs, list(range(16, 20)))
+        gather_words(1, 2560, 3072)
+        gather_scales(2560, 3072)
+        gather_words(2, 2560, 2816)
         gather_words(3, 2560, 2816)
-        multiply(accs[20], 20, 3)
-        multiply(accs[21], 21, 3)
+        first_passes((20, 21), range(4))
         finish(accs, [20, 21])
+        gather_words(2, 2816, 3072)
+        first_passes((23, 22), range(3))
         gather_words(3, 2816, 3072)
         multiply(accs[23], 23, 3)
         multiply(accs[22], 22, 3)
@@ -188,19 +187,14 @@ def tile_moe_tk_lin_relu2_kernel(tc, xT, w_words, w_scales, b, gate, offs, pos1,
         nc.vector.tensor_scalar(last[:], accs[23][:], bias[:, 23:24], 0.0, ADD, MAX)
         nc.vector.tensor_tensor(y[:, 23 * C : 24 * C], last[:], last[:], MULT)
 
-        def pick(r, t0, t1):
-            prod = keep.tile([P, t1 - t0], F32, name=f"prod{r}_{t0}")
-            nc.vector.tensor_tensor(prod[:], y[:].indirect(pos_sb[r][:]), gates[:, r, t0:t1], MULT)
-            return prod
-
-        p = [pick(r, 0, T) for r in range(TOP)]
+        prods = stage.tile([P, TOP, T], F32, name="prods", tag="raw", bufs=3)
+        sums = stage.tile([P, TOP, T], F32, name="sums", tag="raw", bufs=3)
+        for r in range(TOP):
+            nc.vector.tensor_tensor(prods[:, r, :], y[:].indirect(pos_sb[r][:]), gates[:, r, :], MULT)
         cut = 512
-        low = keep.tile([P, T], F32, name="low")
-        high = keep.tile([P, T], F32, name="high")
-        total = keep.tile([P, T], F32, name="total")
-        nc.vector.tensor_tensor(low[:], p[0][:], p[1][:], ADD)
+        nc.vector.tensor_tensor(sums[:, 0, :], prods[:, 0, :], prods[:, 1, :], ADD)
         for t0, t1 in ((0, cut), (cut, T)):
-            nc.vector.tensor_tensor(high[:, t0:t1], p[2][:, t0:t1], p[3][:, t0:t1], ADD)
+            nc.vector.tensor_tensor(sums[:, 1, t0:t1], prods[:, 2, t0:t1], prods[:, 3, t0:t1], ADD)
         for t0, t1 in ((0, cut), (cut, T)):
-            nc.vector.tensor_tensor(total[:, t0:t1], low[:, t0:t1], high[:, t0:t1], ADD)
-            nc.sync.dma_start(out[:, t0:t1], total[:, t0:t1])
+            nc.vector.tensor_tensor(sums[:, 2, t0:t1], sums[:, 0, t0:t1], sums[:, 1, t0:t1], ADD)
+            nc.sync.dma_start(out[:, t0:t1], sums[:, 2, t0:t1])

@@ -20,11 +20,12 @@ P = 128
 K, T, E, C, N, TOP = 2048, 768, 24, 128, 128, 4
 S = E * C
 PASSES = K // 512
+W_SPLIT = 64
 WINDOWS = (2048, 1408, 1408, 1408)
 SCALE_WINDOW = 1408
 FLOPS = 2 * K * N * S
 
-W_EXPERTS = 3
+W_EXPERTS = 6
 
 
 def tile_moe_tk_lin_relu2_kernel(tc, xT, w_words, w_scales, b, gate, offs, pos1, pos2, pos3, pos4, out):
@@ -51,10 +52,29 @@ def tile_moe_tk_lin_relu2_kernel(tc, xT, w_words, w_scales, b, gate, offs, pos1,
             nc.sync.dma_start(head[:], xT[0:512, t0:t1].rearrange("(p j) t -> p j t", j=4))
             heads.append(head)
 
+        half = W_SPLIT * N
+        nc.gpsimd.memset(w_bytes[:, 0 : half // 2].bitcast(I32), 0)
+        nc.vector.memset(w_bytes[:, half // 2 : half].bitcast(I32), 0)
+        nc.gpsimd.memset(w_bytes[:, half : E * PASSES * N].bitcast(I32), 0)
         nc.vector.memset(scales[:].bitcast(I32), 0)
-        nc.gpsimd.memset(w_bytes[:].bitcast(I32), 0)
         for a in range(PASSES):
             nc.vector.memset(words[a][:, T : WINDOWS[a]], 0)
+
+        flat_scales = w_scales.rearrange("e a q n -> q (e a) n").bitcast(I32)
+
+        def load_w_scales(i, m0, m1):
+            for q in range(4):
+                row = 32 * q + i
+                nc.sync.dma_start(
+                    w_bytes[row : row + 1, m0 * N : m1 * N].bitcast(I32).rearrange("q (m n) -> q m n", m=m1 - m0),
+                    flat_scales[4 * q + i : 4 * q + i + 1, m0:m1, :],
+                )
+
+        def load_w(c):
+            nc.sync.dma_start(
+                w_codes[c][:].bitcast(I32).rearrange("p (m n) -> p m n", n=N),
+                w_words[c * W_EXPERTS : (c + 1) * W_EXPERTS].rearrange("e a p n r -> p (e a) (n r)").bitcast(I32),
+            )
 
         nc.sync.dma_start(offs_sb[:], offs)
         raws = [None]
@@ -64,20 +84,23 @@ def tile_moe_tk_lin_relu2_kernel(tc, xT, w_words, w_scales, b, gate, offs, pos1,
             raws.append(raw)
             if a == 1:
                 nc.sync.dma_start(bias[:], b)
-        for q in range(4):
-            nc.sync.dma_start(
-                w_bytes[32 * q : 32 * q + 4, :].bitcast(I32).rearrange("q (m n) -> q m n", m=E * PASSES),
-                w_scales[:, :, 4 * q : 4 * q + 4, :].rearrange("e a q n -> q (e a) n").bitcast(I32),
-            )
-        for c in range(E // W_EXPERTS):
-            nc.sync.dma_start(
-                w_codes[c][:].bitcast(I32).rearrange("p (m n) -> p m n", n=N),
-                w_words[c * W_EXPERTS : (c + 1) * W_EXPERTS].rearrange("e a p n r -> p (e a) (n r)").bitcast(I32),
-            )
+            if a >= 2:
+                load_w_scales(a - 2, 0, W_SPLIT)
+        load_w(0)
+        load_w_scales(2, 0, W_SPLIT)
+        load_w(1)
+        load_w_scales(3, 0, W_SPLIT)
+        load_w(2)
         for r, pos in enumerate((pos1, pos2, pos3, pos4)):
             nc.sync.dma_start(pos_sb[r][:], pos)
+        for i in range(2):
+            load_w_scales(i, W_SPLIT, E * PASSES)
+        load_w(3)
+        for i in range(2, 4):
+            load_w_scales(i, W_SPLIT, E * PASSES)
         gates = stage.tile([P, TOP, T], F32, name="gates", tag="raw", bufs=3)
-        nc.sync.dma_start(gates[:], gate.rearrange("r p t -> p r t"))
+        for r in range(TOP):
+            nc.sync.dma_start(gates[:, r, :], gate[r])
 
         def cast(engine, grouped, raw, t0, t1, base):
             dst = grouped[:, 4 * t0 : 4 * t1].rearrange("p (c i j) -> p c j i", i=4, j=4)

from contextlib import ExitStack

import concourse.mybir as mybir

F32 = mybir.dt.float32
BF16 = mybir.dt.bfloat16
I32 = mybir.dt.int32
U32 = mybir.dt.uint32
U16 = mybir.dt.uint16
U8 = mybir.dt.uint8
FP8X4 = mybir.dt.float8_e4m3fn_x4
COPY = mybir.ActivationFunctionType.Copy
RELU = mybir.ActivationFunctionType.Relu
SQUARE = mybir.ActivationFunctionType.Square
ADD = mybir.AluOpType.add
MULT = mybir.AluOpType.mult
MAX = mybir.AluOpType.max

P = 128
K, T, E, C, N, TOP = 2048, 768, 24, 128, 128, 4
S = E * C
PASSES = K // 512
W_SPLIT = 64
WINDOWS = (2048, 1408, 1408, 1408)
SCALE_WINDOW = 1408
FLOPS = 2 * K * N * S

W_EXPERTS = 6


def tile_moe_tk_lin_relu2_kernel(tc, xT, w_words, w_scales, b, gate, offs, pos1, pos2, pos3, pos4, out):
    nc = tc.nc
    with ExitStack() as ctx:
        keep = ctx.enter_context(tc.tile_pool(name="keep", bufs=1))
        stage = ctx.enter_context(tc.tile_pool(name="stage", bufs=2))
        psum = ctx.enter_context(tc.psum_pool(name="psum", bufs=8))

        offs_sb = keep.tile([P, S // 16], U16, name="offs_sb")
        pos_sb = [keep.tile([P, T // 16], U16, name=f"pos_sb{r}") for r in range(TOP)]
        bias = keep.tile([P, E], F32, name="bias")
        w_codes = [keep.tile([P, W_EXPERTS * PASSES * N * 4], U8, name=f"w_codes{c}", align_bytes=64) for c in range(E // W_EXPERTS)]
        w_bytes = keep.tile([P, E * PASSES * N], U8, name="w_bytes", align_bytes=64)
        words = [keep.tile([P, WINDOWS[a]], I32, name=f"words{a}", align_bytes=64) for a in range(PASSES)]
        scales = keep.tile([P, SCALE_WINDOW], U8, name="scales", align_bytes=64)
        slot_words = [keep.tile([P, S], U32, name=f"slot_words{a}", align_bytes=64) for a in range(PASSES)]
        slot_scales = keep.tile([P, S], U8, name="slot_scales", align_bytes=64)
        y = keep.tile([P, S], F32, name="y")

        heads = []
        for t0, t1 in ((0, 512), (512, T)):
            head = keep.tile([P, 4, t1 - t0], F32, name=f"head{t0}")
            nc.sync.dma_start(head[:], xT[0:512, t0:t1].rearrange("(p j) t -> p j t", j=4))
            heads.append(head)

        half = W_SPLIT * N
        nc.gpsimd.memset(w_bytes[:, 0 : half // 2].bitcast(I32), 0)
        nc.vector.memset(w_bytes[:, half // 2 : half].bitcast(I32), 0)
        nc.gpsimd.memset(w_bytes[:, half : E * PASSES * N].bitcast(I32), 0)
        nc.vector.memset(scales[:].bitcast(I32), 0)
        for a in range(PASSES):
            nc.vector.memset(words[a][:, T : WINDOWS[a]], 0)

        flat_scales = w_scales.rearrange("e a q n -> q (e a) n").bitcast(I32)

        def load_w_scales(i, m0, m1):
            for q in range(4):
                row = 32 * q + i
                nc.sync.dma_start(
                    w_bytes[row : row + 1, m0 * N : m1 * N].bitcast(I32).rearrange("q (m n) -> q m n", m=m1 - m0),
                    flat_scales[4 * q + i : 4 * q + i + 1, m0:m1, :],
                )

        def load_w(c):
            nc.sync.dma_start(
                w_codes[c][:].bitcast(I32).rearrange("p (m n) -> p m n", n=N),
                w_words[c * W_EXPERTS : (c + 1) * W_EXPERTS].rearrange("e a p n r -> p (e a) (n r)").bitcast(I32),
            )

        nc.sync.dma_start(offs_sb[:], offs)
        raws = [None]
        for a in range(1, PASSES):
            raw = stage.tile([P, 4, T], F32, name=f"raw{a}", tag="raw", bufs=3)
            nc.sync.dma_start(raw[:], xT[512 * a : 512 * a + 512, :].rearrange("(p j) t -> p j t", j=4))
            raws.append(raw)
            if a == 1:
                nc.sync.dma_start(bias[:], b)
            if a >= 2:
                load_w_scales(a - 2, 0, W_SPLIT)
        load_w(0)
        load_w_scales(2, 0, W_SPLIT)
        load_w(1)
        load_w_scales(3, 0, W_SPLIT)
        load_w(2)
        for r, pos in enumerate((pos1, pos2, pos3, pos4)):
            nc.sync.dma_start(pos_sb[r][:], pos)
        for i in range(2):
            load_w_scales(i, W_SPLIT, E * PASSES)
        load_w(3)
        for i in range(2, 4):
            load_w_scales(i, W_SPLIT, E * PASSES)
        gates = stage.tile([P, TOP, T], F32, name="gates", tag="raw", bufs=3)
        for r in range(TOP):
            nc.sync.dma_start(gates[:, r, :], gate[r])

        def cast(engine, grouped, raw, t0, t1, base):
            dst = grouped[:, 4 * t0 : 4 * t1].rearrange("p (c i j) -> p c j i", i=4, j=4)
            source = raw[:, :, t0 - base : t1 - base].rearrange("p j (c i) -> p c j i", i=4)
            if engine == "scalar":
                nc.scalar.activation(dst, source, COPY)
            else:
                nc.vector.tensor_copy(dst, source)

        def quantize(a, grouped, t0, t1):
            nc.vector.quantize_mx(
                out=words[a][:, t0:t1].bitcast(FP8X4),
                scales=scales[4 * a : P, t0:t1],
                in_=grouped[:, 4 * t0 : 4 * t1],
            )

        def gather_words(a, s0, s1):
            nc.vector.tensor_copy(
                slot_words[a][:, s0:s1], words[a][:].bitcast(U32).indirect(offs_sb[:, s0 // 16 : s1 // 16])
            )

        def gather_scales(s0, s1):
            nc.vector.tensor_copy(slot_scales[:, s0:s1], scales[:].indirect(offs_sb[:, s0 // 16 : s1 // 16]))

        def multiply(acc, e, a):
            cols = slice(e * C, (e + 1) * C)
            m = (e % W_EXPERTS) * PASSES + a
            nc.tensor.matmul_mx(
                out=acc[:],
                lhsT=w_codes[e // W_EXPERTS][:, m * N * 4 : (m + 1) * N * 4].bitcast(FP8X4),
                lhsT_scale=w_bytes[:, (e * PASSES + a) * N : (e * PASSES + a + 1) * N],
                rhs=slot_words[a][:, cols].bitcast(FP8X4),
                rhs_scale=slot_scales[4 * a : P, cols],
                start=(a == 0),
                stop=(a == PASSES - 1),
            )

        def finish(accs, experts):
            e0 = experts[0]
            relu = stage.tile([P, 4 * C], F32, name="relu")
            for i, e in enumerate(experts):
                nc.scalar.activation(relu[:, i * C : (i + 1) * C], accs[e][:], RELU, bias=bias[:, e : e + 1])
            n = len(experts)
            nc.scalar.activation(y[:, e0 * C : (e0 + n) * C], relu[:, 0 : n * C], SQUARE)

        grouped = stage.tile([P, 4 * T], BF16, name="grouped", align_bytes=64)
        cast("scalar", grouped, heads[0], 0, 160, 0)
        cast("vector", grouped, heads[0], 160, 512, 0)
        quantize(0, grouped, 0, 512)
        cast("vector", grouped, heads[1], 512, 672, 512)
        cast("scalar", grouped, heads[1], 672, 768, 512)
        quantize(0, grouped, 512, 768)
        gather_words(0, 0, 1536)
        gather_words(0, 1536, 3072)

        def cast_and_quantize(a):
            grouped = stage.tile([P, 4 * T], BF16, name="grouped", align_bytes=64)
            cast("scalar", grouped, raws[a], 0, 512, 0)
            cast("scalar", grouped, raws[a], 512, 768, 0)
            quantize(a, grouped, 0, 512)
            quantize(a, grouped, 512, 768)

        accs = {}

        def first_passes(experts, passes):
            for e in experts:
                accs[e] = psum.tile([P, C], F32, name="acc")
                for a in passes:
                    multiply(accs[e], e, a)

        cast_and_quantize(1)
        gather_words(1, 0, 1024)
        cast_and_quantize(2)
        gather_words(1, 1024, 2048)
        gather_words(2, 0, 1024)
        cast_and_quantize(3)
        gather_scales(0, 1024)
        gather_words(3, 0, 1024)
        for e0 in (0, 4):
            first_passes(range(e0, e0 + 4), range(4))
            finish(accs, list(range(e0, e0 + 4)))
        gather_words(2, 1024, 2048)
        gather_scales(1024, 2048)
        gather_words(3, 1024, 2048)
        for e0 in (8, 12):
            first_passes(range(e0, e0 + 4), range(4))
            finish(accs, list(range(e0, e0 + 4)))
        gather_words(1, 2048, 2560)
        gather_words(2, 2048, 2560)
        gather_scales(2048, 2560)
        gather_words(3, 2048, 2560)
        first_passes(range(16, 20), range(4))
        finish(accs, list(range(16, 20)))
        gather_words(1, 2560, 3072)
        gather_scales(2560, 3072)
        gather_words(2, 2560, 2816)
        gather_words(3, 2560, 2816)
        first_passes((20, 21), range(4))
        finish(accs, [20, 21])
        gather_words(2, 2816, 3072)
        first_passes((23, 22), range(3))
        gather_words(3, 2816, 3072)
        multiply(accs[23], 23, 3)
        multiply(accs[22], 22, 3)
        finish(accs, [22])
        last = keep.tile([P, C], F32, name="last")
        nc.vector.tensor_scalar(last[:], accs[23][:], bias[:, 23:24], 0.0, ADD, MAX)
        nc.vector.tensor_tensor(y[:, 23 * C : 24 * C], last[:], last[:], MULT)

        prods = stage.tile([P, TOP, T], F32, name="prods", tag="raw", bufs=3)
        sums = stage.tile([P, TOP, T], F32, name="sums", tag="raw", bufs=3)
        for r in range(TOP):
            nc.vector.tensor_tensor(prods[:, r, :], y[:].indirect(pos_sb[r][:]), gates[:, r, :], MULT)
        cut = 512
        nc.vector.tensor_tensor(sums[:, 0, :], prods[:, 0, :], prods[:, 1, :], ADD)
        for t0, t1 in ((0, cut), (cut, T)):
            nc.vector.tensor_tensor(sums[:, 1, t0:t1], prods[:, 2, t0:t1], prods[:, 3, t0:t1], ADD)
        for t0, t1 in ((0, cut), (cut, T)):
            nc.vector.tensor_tensor(sums[:, 2, t0:t1], sums[:, 0, t0:t1], sums[:, 1, t0:t1], ADD)
            nc.sync.dma_start(out[:, t0:t1], sums[:, 2, t0:t1])
